import numpy as np
import ml_dtypes


def mxq(x, axis, fmt="e4m3"):
    dtype, down = {"e4m3": (ml_dtypes.float8_e4m3fn, 7), "e5m2": (ml_dtypes.float8_e5m2, 14)}[fmt]
    v = np.moveaxis(np.asarray(x, np.float32).astype(ml_dtypes.bfloat16).astype(np.float64), axis, -1)
    blocks = v.reshape(v.shape[:-1] + (-1, 32))
    amax = np.abs(blocks).max(-1, keepdims=True)
    byte = np.maximum(np.where(amax > 0, np.frexp(amax)[1] - 1 + 127, 0) - down, 1)
    scale = np.exp2(byte - 127.0)
    codes = (blocks / scale).astype(np.float32).astype(dtype).astype(np.float64)
    return np.moveaxis((codes * scale).reshape(v.shape), -1, axis)


WIDE = False


def mx_kscale(k):
    if not WIDE:
        return np.ones(k)
    levels = np.array([10, -10, 5, -5, 0])
    if k % 512:
        return np.exp2(np.random.permutation(np.resize(levels, k // 32))).repeat(32)
    a = np.empty((k // 512, 16))
    for p in range(k // 512):
        a[p, :8] = np.random.permutation(np.resize(levels, 8))
        for g in range(8):
            far = levels[np.abs(levels - a[p, g]) >= 10]
            a[p, g + 8] = far[np.random.randint(len(far))]
    return np.exp2(a.ravel()).repeat(32)


def f64(x):
    return np.asarray(x).astype(np.float64)


def striped(idx):
    return np.tile(idx.reshape(-1, 16).T, (8, 1)).astype(np.uint16)


def unstriped(offs):
    return offs[:16].T.reshape(-1).astype(np.int64)


E2M1 = np.array([0.0, 0.5, 1.0, 1.5, 2.0, 3.0, 4.0, 6.0, -0.0, -0.5, -1.0, -1.5, -2.0, -3.0, -4.0, -6.0])


def pack_weight(w, fmt):
    k, n = w.shape
    w = f64(np.asarray(w, np.float32).astype(ml_dtypes.bfloat16)).reshape(k // 32, 32, n)
    amax = np.abs(w).max(1)
    if fmt == "e4m3":
        byte = np.frexp(amax)[1] - 1 + 127 - 7
    else:
        mant, ex = np.frexp(amax / 6.0)
        byte = np.where(mant > 0.5, ex, ex - 1) + 127
    byte = np.clip(np.where(amax > 0, byte, 1), 1, 254)
    scaled = (w * np.exp2(127.0 - byte)[:, None, :]).reshape(k, n).astype(np.float32)
    by_word = np.ascontiguousarray(scaled.reshape(k // 512, 128, 4, n).transpose(0, 1, 3, 2))
    if fmt == "e4m3":
        words = by_word.astype(ml_dtypes.float8_e4m3fn).view(np.uint8)
    else:
        c = by_word.astype(ml_dtypes.float4_e2m1fn).view(np.uint8) & 0xF
        words = (c[..., 0::2] | (c[..., 1::2] << 4)).reshape(k // 512, 128, 2 * n)
    return np.ascontiguousarray(words), np.ascontiguousarray(byte.astype(np.uint8).reshape(k // 512, 16, n))


def unpack_weight(words, scales, fmt):
    g, _, n = scales.shape
    words = np.ascontiguousarray(words).reshape(g, 128, n, -1)
    if fmt == "e4m3":
        vals = words.view(ml_dtypes.float8_e4m3fn).astype(np.float64)
    else:
        nib = np.empty((g, 128, n, 4), np.uint8)
        nib[..., 0::2] = words & 0xF
        nib[..., 1::2] = words >> 4
        vals = E2M1[nib]
    vals = vals * np.repeat(np.exp2(scales.astype(np.float64) - 127.0), 8, axis=1)[..., None]
    return vals.transpose(0, 1, 3, 2).reshape(g * 512, n)


def gelu(v):
    return 0.5 * v * (1.0 + np.tanh(np.sqrt(2.0 / np.pi) * (v + 0.044715 * v**3)))


K, T, S, H, T2, P, N = 512, 4096, 1024, 1024, 2048, 1024, 512

def setup_inputs():
    n = np.random.standard_normal
    s = mx_kscale(K)[:, None]
    u = mx_kscale(H)[:, None]
    d = {}
    d["tab_words"], d["tab_scales"] = pack_weight(n((K, T)) * s, "e4m3")
    d["offs"] = striped(np.random.permutation(T)[:S])
    d["offs2"] = striped(np.random.permutation(T2)[:S])
    d["offs3"] = striped(np.random.permutation(T2)[:P])
    d["offs4"] = striped(np.random.permutation(T2)[:P])
    d["w1"] = (n((K, H)) / s / K ** 0.5).astype(np.float32)
    d["w2_words"], d["w2_scales"] = pack_weight(n((K, H)) / s / K ** 0.5, "e2m1")
    d["gain"] = (np.exp(0.3 * n(H)) * u[:, 0]).astype(np.float32)
    d["wgs"] = np.exp(0.3 * n((128, S))).astype(np.float32)
    d["page0"] = (n((H, T2)) * u).astype(np.float32)
    d["bx"] = (n(H) * u[:, 0]).astype(np.float32)
    d["w3"] = (n((H, N)) / u / H ** 0.5).astype(np.float32)
    d["w4_words"], d["w4_scales"] = pack_weight(n((K, N)) / s / K ** 0.5, "e4m3")
    d["wgo"] = np.exp(0.3 * n((128, P))).astype(np.float32)
    d["page1"] = n((N, T2)).astype(np.float32)
    return d

def reference(tab_words, tab_scales, offs, offs2, offs3, offs4, w1, w2_words, w2_scales, gain, wgs, page0, bx, w3, w4_words, w4_scales, wgo, page1):
    v = unpack_weight(tab_words, tab_scales, "e4m3")[:, unstriped(offs)]
    w2 = unpack_weight(w2_words, w2_scales, "e2m1")
    w4 = unpack_weight(w4_words, w4_scales, "e4m3")
    a = mxq(f64(w1), 0, "e4m3").T @ v
    b = w2.T @ v
    h = f64(gain)[:, None] * (a - np.abs(b))
    page = f64(page0).copy()
    page[:, unstriped(offs2)] = np.tile(f64(wgs), (H // 128, 1)) * h
    x = page[:, unstriped(offs3)] + f64(bx)[:, None]
    m = mxq(f64(w3), 0, "e4m3").T @ mxq(x, 0, "e4m3")
    q = w4.T @ v
    y = m * q + m
    out = f64(page1).copy()
    out[:, unstriped(offs4)] = np.tile(f64(wgo), (N // 128, 1)) * y
    return out

@@ -1,0 +1,328 @@
+from contextlib import ExitStack
+
+import concourse.mybir as mybir
+from concourse.masks import make_identity
+
+K, T, S, H, T2, N = 512, 4096, 1024, 1024, 2048, 512
+FLOPS = 2 * K * H * S * 2 + 2 * H * N * S + 2 * K * N * S
+
+F32 = mybir.dt.float32
+BF16 = mybir.dt.bfloat16
+I32 = mybir.dt.int32
+U32 = mybir.dt.uint32
+U16 = mybir.dt.uint16
+U8 = mybir.dt.uint8
+FP8X4 = mybir.dt.float8_e4m3fn_x4
+FP4X4 = mybir.dt.float4_e2m1fn_x4
+ACT = mybir.ActivationFunctionType
+ALU = mybir.AluOpType
+
+P = 128
+PACK = 4
+KP = P * PACK
+HALF = 512
+LIST_COLS = S // 16
+HALF_COLS = HALF // 16
+
+
+def tile_list_cue_drill_page_kernel(
+    tc, tab_words, tab_scales, offs, offs2, offs3, offs4, w1, w2_words, w2_scales,
+    gain, wgs, page0, bx, w3, w4_words, w4_scales, wgo, page1, out,
+):
+    nc = tc.nc
+    with ExitStack() as ctx:
+        keep = ctx.enter_context(tc.tile_pool(name="keep", bufs=1))
+        psum = ctx.enter_context(tc.psum_pool(name="psum", bufs=2))
+
+        def half_list(lst, hf):
+            return lst[:, hf * HALF_COLS:(hf + 1) * HALF_COLS]
+
+        def load_scale_rows(queue, plane, rows):
+            for q in range(4):
+                queue.dma_start(out=plane[32 * q:32 * q + 4, :].bitcast(I32), in_=rows[0, 4 * q:4 * q + 4, :].bitcast(I32))
+
+        tab_s_rows = keep.tile([P, T], U8, name="tab_s_rows", align_bytes=64)
+        tab_s = keep.tile([P, T], U8, name="tab_s", align_bytes=64)
+        w2_s_raw = keep.tile([P, H], U8, name="w2_s_raw", align_bytes=64)
+        w4_s = keep.tile([P, N], U8, name="w4_s", align_bytes=64)
+        nc.gpsimd.memset(w2_s_raw[:].bitcast(I32), 0)
+        nc.vector.memset(tab_s[:].bitcast(I32), 0)
+        nc.gpsimd.memset(w4_s[:].bitcast(I32), 0)
+        ident = keep.tile([P, P], F32, name="ident", align_bytes=64)
+        make_identity(nc, ident[:])
+
+        lst1 = keep.tile([P, LIST_COLS], U16, name="lst1")
+        lst2 = keep.tile([P, LIST_COLS], U16, name="lst2")
+        lst3 = keep.tile([P, LIST_COLS], U16, name="lst3")
+        lst4 = keep.tile([P, LIST_COLS], U16, name="lst4")
+        gain_sb = keep.tile([P, 2, PACK], F32, name="gain_sb")
+        bx_sb = keep.tile([P, 2, PACK], F32, name="bx_sb")
+        load_scale_rows(nc.sync, tab_s_rows, tab_scales)
+
+        def load_w(w, b, cols, name):
+            raw = keep.tile([P, PACK, KP], F32, name=name, tag="w_rows", bufs=2, align_bytes=64)
+            nc.sync.dma_start(out=raw[:], in_=w[b * KP:(b + 1) * KP, cols].rearrange("(p j) c -> p j c", j=PACK))
+            return raw
+
+        def load_page0(i):
+            b, t = divmod(i, PACK)
+            pg = keep.tile([P, T2], F32, name="pg%d" % i, tag="page", bufs=7, align_bytes=64)
+            nc.sync.dma_start(out=pg[:], in_=page0[b * KP:(b + 1) * KP, :].rearrange("(p t) c -> t p c", t=PACK)[t])
+            return pg
+
+        w1_raw = [load_w(w1, 0, slice(0, KP), "w1_raw0")]
+        w2_raw = keep.tile([P, 2 * H], U8, name="w2_raw", align_bytes=64)
+        nc.sync.dma_start(out=w2_raw[:].bitcast(I32), in_=w2_words[0].bitcast(I32))
+        load_scale_rows(nc.sync, w2_s_raw, w2_scales)
+        nc.sync.dma_start(lst1[:], offs)
+        tab_w = keep.tile([P, T], U32, name="tab_w", align_bytes=64)
+        nc.sync.dma_start(out=tab_w[:].bitcast(I32), in_=tab_words[0].rearrange("p c i -> p (c i)").bitcast(I32))
+        pages = [load_page0(0)]
+        nc.sync.dma_start(out=gain_sb[:], in_=gain.rearrange("(b p t) -> p b t", b=2, t=PACK))
+        nc.sync.dma_start(lst2[:], offs2)
+        wgs_rows = wgs.rearrange("(m t) j -> m t j", t=PACK)
+        wgs_sb = []
+
+        def load_wgs(t0, t1):
+            dealt = keep.tile([P, t1 - t0, S], F32, name="wgs%d" % t0, align_bytes=64)
+            for q in range(4):
+                nc.sync.dma_start(out=dealt[32 * q:32 * q + 32, :, :], in_=wgs_rows[:, t0:t1, :])
+            wgs_sb.extend(dealt[:, t, :] for t in range(t1 - t0))
+
+        load_wgs(0, 1)
+        pages.append(load_page0(1))
+        load_wgs(1, 2)
+        w1_raw.append(load_w(w1, 0, slice(KP, 2 * KP), "w1_raw1"))
+        nc.sync.dma_start(lst3[:], offs3)
+        nc.sync.dma_start(out=bx_sb[:], in_=bx.rearrange("(b p t) -> p b t", b=2, t=PACK))
+        pages.append(load_page0(2))
+        load_wgs(2, 4)
+        pages.append(load_page0(3))
+        load_scale_rows(nc.sync, w4_s, w4_scales)
+        w4_w = keep.tile([P, N], U32, name="w4_w", align_bytes=64)
+        nc.sync.dma_start(out=w4_w[:].bitcast(I32), in_=w4_words[0].rearrange("p c i -> p (c i)").bitcast(I32))
+        wgo_sb = keep.tile([P, S], F32, name="wgo_sb", align_bytes=64)
+        nc.sync.dma_start(out=wgo_sb[:], in_=wgo)
+        nc.sync.dma_start(lst4[:], offs4)
+        for i in range(4, 7):
+            pages.append(load_page0(i))
+
+        for q in range(4):
+            nc.vector.tensor_copy(tab_s[32 * q:32 * q + 4, :].bitcast(I32), tab_s_rows[32 * q:32 * q + 4, :].bitcast(I32))
+        v_s = keep.tile([P, S], U8, name="v_s", align_bytes=64)
+        nc.vector.tensor_copy(v_s[:], tab_s[:].indirect(lst1[:]))
+
+        w2_w = keep.tile([P, 2 * H], U8, name="w2_w", align_bytes=64)
+        w2_s = keep.tile([P, H], U8, name="w2_s", align_bytes=64)
+        w1_w, w1_s, w3_w, w3_s = [], [], [], []
+
+        def deal_w2_words(b):
+            nc.vector.tensor_copy(
+                out=w2_w[:, 2 * KP * b:2 * KP * (b + 1)].rearrange("p (t m e) -> p t m e", t=PACK, e=2),
+                in_=w2_raw[:, 2 * KP * b:2 * KP * (b + 1)].rearrange("p (m t e) -> p t m e", t=PACK, e=2))
+
+        def deal_w2_scales(b):
+            nc.vector.tensor_copy(
+                out=w2_s[:, KP * b:KP * (b + 1)].rearrange("p (t m) -> p t m", t=PACK),
+                in_=w2_s_raw[:, KP * b:KP * (b + 1)].rearrange("p (m t) -> p t m", t=PACK))
+
+        def quantise(grouped, name):
+            codes = keep.tile([P, KP], U32, name=name + "_w", align_bytes=64)
+            scales = keep.tile([P, KP], U8, name=name + "_s", align_bytes=64)
+            nc.vector.quantize_mx(out=codes[:].bitcast(FP8X4), scales=scales[:], in_=grouped[:])
+            return codes, scales
+
+        def make_w1(b):
+            grouped = keep.tile([P, PACK * KP], BF16, name="w1_bf%d" % b, tag="w_bf", bufs=3, align_bytes=64)
+            nc.scalar.copy(out=grouped[:].rearrange("p (t m j) -> p m t j", t=PACK, j=PACK),
+                           in_=w1_raw[b][:].rearrange("p j (m t) -> p m t j", t=PACK))
+            codes, scales = quantise(grouped, "w1_%d" % b)
+            w1_w.append(codes)
+            w1_s.append(scales)
+
+        def make_w3(b):
+            raw = load_w(w3, b, slice(0, N), "w3_raw%d" % b)
+            grouped = keep.tile([P, PACK * KP], BF16, name="w3_bf%d" % b, tag="w_bf", bufs=3, align_bytes=64)
+            nc.scalar.copy(out=grouped[:].rearrange("p (c i j) -> p c j i", i=4, j=PACK),
+                           in_=raw[:].rearrange("p j (c i) -> p c j i", i=4))
+            codes, scales = quantise(grouped, "w3_%d" % b)
+            w3_w.append(codes)
+            w3_s.append(scales)
+
+        make_w1(0)
+        deal_w2_words(0)
+        deal_w2_scales(0)
+        neg_gain = keep.tile([P, 2, PACK], F32, name="neg_gain")
+        v_w = []
+        for hf in range(2):
+            vw = keep.tile([P, HALF], U32, name="v_w%d" % hf, align_bytes=64)
+            nc.vector.tensor_copy(vw[:], tab_w[:].indirect(half_list(lst1, hf)))
+            v_w.append(vw)
+        nc.vector.tensor_scalar_mul(neg_gain[:], gain_sb[:], -1.0)
+        deal_w2_words(1)
+        deal_w2_scales(1)
+        stage = [keep.tile([P, 2 * HALF], F32, name="stage%d" % hf, align_bytes=64) for hf in range(2)]
+
+        hs = {}
+
+        def make_h(i, hf):
+            b, t = divmod(i, PACK)
+            if hf == 0 and i == 7:
+                hs[i] = keep.tile([P, S], F32, name="h7", align_bytes=64)
+            elif hf == 0:
+                hs[i] = keep.tile([P, S], F32, name="h%d" % i, tag="h", bufs=3, align_bytes=64)
+            h = hs[i]
+            rows = slice(t * P, (t + 1) * P)
+            a_ps = psum.tile([P, HALF], F32, name="a_ps")
+            b_ps = psum.tile([P, HALF], F32, name="b_ps")
+            for jj in range(4):
+                js = slice(jj * P, (jj + 1) * P)
+                vs = v_s[:, hf * HALF + jj * P: hf * HALF + (jj + 1) * P]
+                nc.tensor.matmul_mx(out=a_ps[:, js], lhsT=v_w[hf][:, js].bitcast(FP8X4), lhsT_scale=vs,
+                                    rhs=w1_w[b][:, rows].bitcast(FP8X4), rhs_scale=w1_s[b][:, rows],
+                                    start=True, stop=True)
+            for jj in range(4):
+                js = slice(jj * P, (jj + 1) * P)
+                vs = v_s[:, hf * HALF + jj * P: hf * HALF + (jj + 1) * P]
+                c0 = b * KP + t * P
+                nc.tensor.matmul_mx(out=b_ps[:, js], lhsT=v_w[hf][:, js].bitcast(FP8X4), lhsT_scale=vs,
+                                    rhs=w2_w[:, 2 * c0:2 * (c0 + P)].bitcast(FP4X4), rhs_scale=w2_s[:, c0:c0 + P],
+                                    start=True, stop=True)
+            a_t = stage[hf][:, 0:HALF]
+            b_t = stage[hf][:, HALF:2 * HALF]
+            nc.scalar.activation(a_t, a_ps[:], ACT.Copy, scale=-1.0)
+            nc.scalar.activation(b_t, b_ps[:], ACT.Abs)
+            h_ps = psum.tile([P, HALF], F32, name="h_ps")
+            for jj in range(4):
+                js = slice(jj * P, (jj + 1) * P)
+                nc.tensor.matmul(h_ps[:, js], lhsT=a_t[:, js], rhs=ident[:], is_transpose=True, start=True, stop=False)
+                nc.tensor.matmul(h_ps[:, js], lhsT=b_t[:, js], rhs=ident[:], is_transpose=True, start=False, stop=True)
+            nc.scalar.activation(h[:, hf * HALF:(hf + 1) * HALF], h_ps[:], ACT.Copy, scale=neg_gain[:, b, t:t + 1])
+
+        make_h(0, 0)
+        make_h(0, 1)
+
+        planes = {}
+        x_bf = [keep.tile([P, PACK * HALF], BF16, name="x_bf%d" % hf, align_bytes=64) for hf in range(2)]
+        x_w, x_s = {}, {}
+
+        def plane_tile(b, hf):
+            if (b, hf) not in planes:
+                planes[(b, hf)] = keep.tile([P, PACK, HALF], BF16, name="planes%d%d" % (b, hf), tag="planes", bufs=3, align_bytes=64)
+            return planes[(b, hf)]
+
+        def add_bias(i, hf, picked):
+            b, t = divmod(i, PACK)
+            nc.scalar.activation(plane_tile(b, hf)[:, t, :], picked, ACT.Identity, bias=bx_sb[:, b, t:t + 1])
+
+        def make_x(b, hf):
+            grouped = x_bf[hf]
+            nc.scalar.copy(out=grouped[:].rearrange("p (c i t) -> p c t i", i=4, t=PACK),
+                           in_=planes[(b, hf)][:].rearrange("p t (c i) -> p c t i", i=4))
+            x_w[(b, hf)], x_s[(b, hf)] = quantise(grouped, "x_%d%d" % (b, hf))
+
+        drill = []
+
+        def load_page1(nt):
+            tag, bufs = ("w_rows", 2) if nt < 2 else ("page", 7)
+            pg = keep.tile([P, T2], F32, name="drill%d" % nt, tag=tag, bufs=bufs, align_bytes=64)
+            nc.sync.dma_start(out=pg[:], in_=page1[nt * P:(nt + 1) * P, :])
+            drill.append(pg)
+
+        def put_h(i):
+            t = i % PACK
+            if i == 0:
+                for hf in range(2):
+                    js = slice(hf * HALF, (hf + 1) * HALF)
+                    nc.vector.tensor_tensor(pages[i][:].indirect(half_list(lst2, hf)), hs[i][:, js], wgs_sb[t][:, js], ALU.mult)
+            else:
+                nc.vector.tensor_tensor(pages[i][:].indirect(lst2[:]), hs[i][:], wgs_sb[t], ALU.mult)
+
+        def pick_x(i):
+            if i < PACK:
+                nc.vector.tensor_copy(stage[1][:], pages[i][:].indirect(lst3[:]))
+                for hf in range(2):
+                    add_bias(i, hf, stage[1][:, hf * HALF:(hf + 1) * HALF])
+            else:
+                picked = stage[1][:, (i % 2) * HALF:(i % 2 + 1) * HALF]
+                nc.vector.tensor_copy(picked, pages[i][:].indirect(half_list(lst3, 0)))
+                add_bias(i, 0, picked)
+            if i == 0:
+                pages.append(load_page0(7))
+
+        qw = []
+
+        def make_q(nt):
+            ns = slice(nt * P, (nt + 1) * P)
+            q1 = keep.tile([P, S], F32, name="q1_%d" % nt, align_bytes=64)
+            for hf in range(2):
+                js = slice(hf * HALF, (hf + 1) * HALF)
+                q_ps = psum.tile([P, HALF], F32, name="q_ps", tag="out_ps")
+                nc.tensor.matmul_mx(out=q_ps[:], lhsT=w4_w[:, ns].bitcast(FP8X4), lhsT_scale=w4_s[:, ns],
+                                    rhs=v_w[hf][:].bitcast(FP8X4), rhs_scale=v_s[:, js], start=True, stop=True)
+                nc.scalar.activation(q1[:, js], q_ps[:], ACT.Copy, bias=1.0)
+            return q1
+
+        def make_qw(q1, dst):
+            nc.vector.tensor_tensor(dst, q1[:], wgo_sb[:], ALU.mult)
+            qw.append(dst)
+
+        make_h(1, 0)
+        make_h(1, 1)
+        put_h(0)
+        make_w1(1)
+        make_h(2, 0)
+        make_h(2, 1)
+        put_h(1)
+        for i in range(2, 8):
+            if i < 7:
+                make_h(i + 1, 0)
+            if i in (2, 3, 4):
+                q1 = make_q(i - 2)
+                make_qw(q1, q1[:])
+            if i in (3, 4):
+                make_w3(i - 3)
+            if i == 5:
+                q1_last = make_q(3)
+            if i in (6, 7):
+                make_x(0, i - 6)
+            pick_x(i - 2)
+            if i < 7:
+                make_h(i + 1, 1)
+            put_h(i)
+            if i >= 4:
+                load_page1(i - 4)
+        pick_x(6)
+        pick_x(7)
+
+        make_x(1, 0)
+        late_b = x_bf[0][:].bitcast(F32)
+        late = [hs[7][:, 0:HALF], hs[7][:, HALF:S], late_b[:, 0:HALF], late_b[:, HALF:S]]
+        for t in range(4):
+            nc.vector.tensor_copy(late[t], pages[4 + t][:].indirect(half_list(lst3, 1)))
+            if t == 1:
+                make_qw(q1_last, wgs_sb[3])
+
+        def put_y(nt, hf):
+            ns = slice(nt * P, (nt + 1) * P)
+            js = slice(hf * HALF, (hf + 1) * HALF)
+            m_ps = psum.tile([P, HALF], F32, name="m_ps", tag="out_ps")
+            for b in (1, 0):
+                nc.tensor.matmul_mx(out=m_ps[:], lhsT=w3_w[b][:, ns].bitcast(FP8X4), lhsT_scale=w3_s[b][:, ns],
+                                    rhs=x_w[(b, hf)][:].bitcast(FP8X4), rhs_scale=x_s[(b, hf)][:],
+                                    start=(b == 1), stop=(b == 0))
+            m_sb = keep.tile([P, HALF], F32, name="m_sb", tag="m_sb", bufs=3, align_bytes=64)
+            nc.scalar.copy(m_sb[:], m_ps[:])
+            nc.vector.tensor_tensor(drill[nt][:].indirect(half_list(lst4, hf)), m_sb[:], qw[nt][:, js], ALU.mult)
+
+        put_y(0, 0)
+        put_y(1, 0)
+        for t in range(4):
+            add_bias(4 + t, 1, late[t])
+        make_x(1, 1)
+        put_y(2, 0)
+        for nt in range(4):
+            if nt == 1:
+                put_y(3, 0)
+            put_y(nt, 1)
+            nc.sync.dma_start(out=out[nt * P:(nt + 1) * P, :], in_=drill[nt][:])

@@ -77,9 +77,9 @@ def tile_list_cue_drill_page_kernel(
         nc.sync.dma_start(lst1[:], offs)
         tab_w = keep.tile([P, T], U32, name="tab_w", align_bytes=64)
         nc.sync.dma_start(out=tab_w[:].bitcast(I32), in_=tab_words[0].rearrange("p c i -> p (c i)").bitcast(I32))
-        pages = [load_page0(0)]
         nc.sync.dma_start(out=gain_sb[:], in_=gain.rearrange("(b p t) -> p b t", b=2, t=PACK))
         nc.sync.dma_start(lst2[:], offs2)
+        pages = [load_page0(0)]
         wgs_rows = wgs.rearrange("(m t) j -> m t j", t=PACK)
         wgs_sb = []
 
@@ -158,9 +158,8 @@ def tile_list_cue_drill_page_kernel(
             vw = keep.tile([P, HALF], U32, name="v_w%d" % hf, align_bytes=64)
             nc.vector.tensor_copy(vw[:], tab_w[:].indirect(half_list(lst1, hf)))
             v_w.append(vw)
-        nc.vector.tensor_scalar_mul(neg_gain[:], gain_sb[:], -1.0)
-        deal_w2_words(1)
-        deal_w2_scales(1)
+            if hf == 0:
+                nc.vector.tensor_scalar_mul(neg_gain[:], gain_sb[:], -1.0)
         stage = [keep.tile([P, 2 * HALF], F32, name="stage%d" % hf, align_bytes=64) for hf in range(2)]
 
         hs = {}
@@ -192,31 +191,52 @@ def tile_list_cue_drill_page_kernel(
             b_t = stage[hf][:, HALF:2 * HALF]
             nc.scalar.activation(a_t, a_ps[:], ACT.Copy, scale=-1.0)
             nc.scalar.activation(b_t, b_ps[:], ACT.Abs)
-            h_ps = psum.tile([P, HALF], F32, name="h_ps")
+            h_ps = psum.tile([P, HALF], F32, name="h_ps", tag="h_ps")
             for jj in range(4):
                 js = slice(jj * P, (jj + 1) * P)
                 nc.tensor.matmul(h_ps[:, js], lhsT=a_t[:, js], rhs=ident[:], is_transpose=True, start=True, stop=False)
                 nc.tensor.matmul(h_ps[:, js], lhsT=b_t[:, js], rhs=ident[:], is_transpose=True, start=False, stop=True)
             nc.scalar.activation(h[:, hf * HALF:(hf + 1) * HALF], h_ps[:], ACT.Copy, scale=neg_gain[:, b, t:t + 1])
 
-        make_h(0, 0)
-        make_h(0, 1)
+        def make_first_h(hf):
+            js = slice(hf * HALF, (hf + 1) * HALF)
+            tag = ("out_ps", "h_ps")[hf]
+            a_ps = psum.tile([P, HALF], F32, name="a_first", tag=tag)
+            b_ps = psum.tile([P, HALF], F32, name="b_first", tag=tag)
+            nc.tensor.matmul_mx(out=a_ps[:], lhsT=w1_w[0][:, 0:P].bitcast(FP8X4), lhsT_scale=w1_s[0][:, 0:P],
+                                rhs=v_w[hf][:].bitcast(FP8X4), rhs_scale=v_s[:, js], start=True, stop=True)
+            nc.tensor.matmul_mx(out=b_ps[:], lhsT=w2_w[:, 0:2 * P].bitcast(FP4X4), lhsT_scale=w2_s[:, 0:P],
+                                rhs=v_w[hf][:].bitcast(FP8X4), rhs_scale=v_s[:, js], start=True, stop=True)
+            gain_a = stage[hf][:, 0:HALF]
+            abs_b = stage[hf][:, HALF:2 * HALF]
+            nc.scalar.activation(gain_a, a_ps[:], ACT.Copy, scale=gain_sb[:, 0, 0:1])
+            nc.scalar.activation(abs_b, b_ps[:], ACT.Abs)
+            nc.vector.scalar_tensor_tensor(out=hs[0][:, js], in0=abs_b, scalar=neg_gain[:, 0, 0:1], in1=gain_a,
+                                           op0=ALU.mult, op1=ALU.add)
+
+        hs[0] = keep.tile([P, S], F32, name="h0", tag="h", bufs=3, align_bytes=64)
+        make_first_h(0)
+        make_first_h(1)
 
         planes = {}
-        x_bf = [keep.tile([P, PACK * HALF], BF16, name="x_bf%d" % hf, align_bytes=64) for hf in range(2)]
+        x_late = keep.tile([P, PACK * HALF], BF16, name="x_late", align_bytes=64)
         x_w, x_s = {}, {}
 
         def plane_tile(b, hf):
             if (b, hf) not in planes:
-                planes[(b, hf)] = keep.tile([P, PACK, HALF], BF16, name="planes%d%d" % (b, hf), tag="planes", bufs=3, align_bytes=64)
+                planes[(b, hf)] = keep.tile([P, PACK, HALF], BF16, name="planes%d%d" % (b, hf), tag="planes", bufs=2, align_bytes=64)
             return planes[(b, hf)]
 
         def add_bias(i, hf, picked):
             b, t = divmod(i, PACK)
-            nc.scalar.activation(plane_tile(b, hf)[:, t, :], picked, ACT.Identity, bias=bx_sb[:, b, t:t + 1])
+            if (b, hf) == (1, 0):
+                dst = x_late[:].rearrange("p (n t) -> p t n", t=PACK)[:, t, :]
+            else:
+                dst = plane_tile(b, hf)[:, t, :]
+            nc.scalar.activation(dst, picked, ACT.Identity, bias=bx_sb[:, b, t:t + 1])
 
         def make_x(b, hf):
-            grouped = x_bf[hf]
+            grouped = keep.tile([P, PACK * HALF], BF16, name="x_bf%d%d" % (b, hf), tag="x_bf", bufs=2, align_bytes=64)
             nc.scalar.copy(out=grouped[:].rearrange("p (c i t) -> p c t i", i=4, t=PACK),
                            in_=planes[(b, hf)][:].rearrange("p t (c i) -> p c t i", i=4))
             x_w[(b, hf)], x_s[(b, hf)] = quantise(grouped, "x_%d%d" % (b, hf))
@@ -270,6 +290,8 @@ def tile_list_cue_drill_page_kernel(
         make_h(1, 0)
         make_h(1, 1)
         put_h(0)
+        deal_w2_words(1)
+        deal_w2_scales(1)
         make_w1(1)
         make_h(2, 0)
         make_h(2, 1)
@@ -277,40 +299,38 @@ def tile_list_cue_drill_page_kernel(
         for i in range(2, 8):
             if i < 7:
                 make_h(i + 1, 0)
-            if i in (2, 3, 4):
-                q1 = make_q(i - 2)
-                make_qw(q1, q1[:])
-            if i in (3, 4):
-                make_w3(i - 3)
-            if i == 5:
-                q1_last = make_q(3)
             if i in (6, 7):
                 make_x(0, i - 6)
             pick_x(i - 2)
             if i < 7:
                 make_h(i + 1, 1)
             put_h(i)
-            if i >= 4:
-                load_page1(i - 4)
+        for nt in range(3):
+            q1 = make_q(nt)
+            make_qw(q1, q1[:])
+        q1_last = make_q(3)
+        make_w3(0)
+        make_w3(1)
+        for nt in range(4):
+            load_page1(nt)
         pick_x(6)
         pick_x(7)
 
-        make_x(1, 0)
-        late_b = x_bf[0][:].bitcast(F32)
+        x_w[(1, 0)], x_s[(1, 0)] = quantise(x_late, "x_10")
+        late_b = x_late[:].bitcast(F32)
         late = [hs[7][:, 0:HALF], hs[7][:, HALF:S], late_b[:, 0:HALF], late_b[:, HALF:S]]
         for t in range(4):
             nc.vector.tensor_copy(late[t], pages[4 + t][:].indirect(half_list(lst3, 1)))
-            if t == 1:
-                make_qw(q1_last, wgs_sb[3])
+        make_qw(q1_last, wgs_sb[3])
 
         def put_y(nt, hf):
             ns = slice(nt * P, (nt + 1) * P)
             js = slice(hf * HALF, (hf + 1) * HALF)
-            m_ps = psum.tile([P, HALF], F32, name="m_ps", tag="out_ps")
-            for b in (1, 0):
+            m_ps = psum.tile([P, HALF], F32, name="m_ps", tag="h_ps")
+            for b in range(2):
                 nc.tensor.matmul_mx(out=m_ps[:], lhsT=w3_w[b][:, ns].bitcast(FP8X4), lhsT_scale=w3_s[b][:, ns],
                                     rhs=x_w[(b, hf)][:].bitcast(FP8X4), rhs_scale=x_s[(b, hf)][:],
-                                    start=(b == 1), stop=(b == 0))
+                                    start=(b == 0), stop=(b == 1))
             m_sb = keep.tile([P, HALF], F32, name="m_sb", tag="m_sb", bufs=3, align_bytes=64)
             nc.scalar.copy(m_sb[:], m_ps[:])
             nc.vector.tensor_tensor(drill[nt][:].indirect(half_list(lst4, hf)), m_sb[:], qw[nt][:, js], ALU.mult)

from contextlib import ExitStack

import concourse.mybir as mybir
from concourse.masks import make_identity

K, T, S, H, T2, N = 512, 4096, 1024, 1024, 2048, 512
FLOPS = 2 * K * H * S * 2 + 2 * H * N * S + 2 * K * N * S

F32 = mybir.dt.float32
BF16 = mybir.dt.bfloat16
I32 = mybir.dt.int32
U32 = mybir.dt.uint32
U16 = mybir.dt.uint16
U8 = mybir.dt.uint8
FP8X4 = mybir.dt.float8_e4m3fn_x4
FP4X4 = mybir.dt.float4_e2m1fn_x4
ACT = mybir.ActivationFunctionType
ALU = mybir.AluOpType

P = 128
PACK = 4
KP = P * PACK
HALF = 512
LIST_COLS = S // 16
HALF_COLS = HALF // 16


def tile_list_cue_drill_page_kernel(
    tc, tab_words, tab_scales, offs, offs2, offs3, offs4, w1, w2_words, w2_scales,
    gain, wgs, page0, bx, w3, w4_words, w4_scales, wgo, page1, out,
):
    nc = tc.nc
    with ExitStack() as ctx:
        keep = ctx.enter_context(tc.tile_pool(name="keep", bufs=1))
        psum = ctx.enter_context(tc.psum_pool(name="psum", bufs=2))

        def half_list(lst, hf):
            return lst[:, hf * HALF_COLS:(hf + 1) * HALF_COLS]

        def load_scale_rows(queue, plane, rows):
            for q in range(4):
                queue.dma_start(out=plane[32 * q:32 * q + 4, :].bitcast(I32), in_=rows[0, 4 * q:4 * q + 4, :].bitcast(I32))

        tab_s_rows = keep.tile([P, T], U8, name="tab_s_rows", align_bytes=64)
        tab_s = keep.tile([P, T], U8, name="tab_s", align_bytes=64)
        w2_s_raw = keep.tile([P, H], U8, name="w2_s_raw", align_bytes=64)
        w4_s = keep.tile([P, N], U8, name="w4_s", align_bytes=64)
        nc.gpsimd.memset(w2_s_raw[:].bitcast(I32), 0)
        nc.vector.memset(tab_s[:].bitcast(I32), 0)
        nc.gpsimd.memset(w4_s[:].bitcast(I32), 0)
        ident = keep.tile([P, P], F32, name="ident", align_bytes=64)
        make_identity(nc, ident[:])

        lst1 = keep.tile([P, LIST_COLS], U16, name="lst1")
        lst2 = keep.tile([P, LIST_COLS], U16, name="lst2")
        lst3 = keep.tile([P, LIST_COLS], U16, name="lst3")
        lst4 = keep.tile([P, LIST_COLS], U16, name="lst4")
        gain_sb = keep.tile([P, 2, PACK], F32, name="gain_sb")
        bx_sb = keep.tile([P, 2, PACK], F32, name="bx_sb")
        load_scale_rows(nc.sync, tab_s_rows, tab_scales)

        def load_w(w, b, cols, name):
            raw = keep.tile([P, PACK, KP], F32, name=name, tag="w_rows", bufs=2, align_bytes=64)
            nc.sync.dma_start(out=raw[:], in_=w[b * KP:(b + 1) * KP, cols].rearrange("(p j) c -> p j c", j=PACK))
            return raw

        def load_page0(i):
            b, t = divmod(i, PACK)
            pg = keep.tile([P, T2], F32, name="pg%d" % i, tag="page", bufs=7, align_bytes=64)
            nc.sync.dma_start(out=pg[:], in_=page0[b * KP:(b + 1) * KP, :].rearrange("(p t) c -> t p c", t=PACK)[t])
            return pg

        w1_raw = [load_w(w1, 0, slice(0, KP), "w1_raw0")]
        w2_raw = keep.tile([P, 2 * H], U8, name="w2_raw", align_bytes=64)
        nc.sync.dma_start(out=w2_raw[:].bitcast(I32), in_=w2_words[0].bitcast(I32))
        load_scale_rows(nc.sync, w2_s_raw, w2_scales)
        nc.sync.dma_start(lst1[:], offs)
        tab_w = keep.tile([P, T], U32, name="tab_w", align_bytes=64)
        nc.sync.dma_start(out=tab_w[:].bitcast(I32), in_=tab_words[0].rearrange("p c i -> p (c i)").bitcast(I32))
        nc.sync.dma_start(out=gain_sb[:], in_=gain.rearrange("(b p t) -> p b t", b=2, t=PACK))
        nc.sync.dma_start(lst2[:], offs2)
        pages = [load_page0(0)]
        wgs_rows = wgs.rearrange("(m t) j -> m t j", t=PACK)
        wgs_sb = []

        def load_wgs(t0, t1):
            dealt = keep.tile([P, t1 - t0, S], F32, name="wgs%d" % t0, align_bytes=64)
            for q in range(4):
                nc.sync.dma_start(out=dealt[32 * q:32 * q + 32, :, :], in_=wgs_rows[:, t0:t1, :])
            wgs_sb.extend(dealt[:, t, :] for t in range(t1 - t0))

        load_wgs(0, 1)
        pages.append(load_page0(1))
        load_wgs(1, 2)
        w1_raw.append(load_w(w1, 0, slice(KP, 2 * KP), "w1_raw1"))
        nc.sync.dma_start(lst3[:], offs3)
        nc.sync.dma_start(out=bx_sb[:], in_=bx.rearrange("(b p t) -> p b t", b=2, t=PACK))
        pages.append(load_page0(2))
        load_wgs(2, 4)
        pages.append(load_page0(3))
        load_scale_rows(nc.sync, w4_s, w4_scales)
        w4_w = keep.tile([P, N], U32, name="w4_w", align_bytes=64)
        nc.sync.dma_start(out=w4_w[:].bitcast(I32), in_=w4_words[0].rearrange("p c i -> p (c i)").bitcast(I32))
        wgo_sb = keep.tile([P, S], F32, name="wgo_sb", align_bytes=64)
        nc.sync.dma_start(out=wgo_sb[:], in_=wgo)
        nc.sync.dma_start(lst4[:], offs4)
        for i in range(4, 7):
            pages.append(load_page0(i))

        for q in range(4):
            nc.vector.tensor_copy(tab_s[32 * q:32 * q + 4, :].bitcast(I32), tab_s_rows[32 * q:32 * q + 4, :].bitcast(I32))
        v_s = keep.tile([P, S], U8, name="v_s", align_bytes=64)
        nc.vector.tensor_copy(v_s[:], tab_s[:].indirect(lst1[:]))

        w2_w = keep.tile([P, 2 * H], U8, name="w2_w", align_bytes=64)
        w2_s = keep.tile([P, H], U8, name="w2_s", align_bytes=64)
        w1_w, w1_s, w3_w, w3_s = [], [], [], []

        def deal_w2_words(b):
            nc.vector.tensor_copy(
                out=w2_w[:, 2 * KP * b:2 * KP * (b + 1)].rearrange("p (t m e) -> p t m e", t=PACK, e=2),
                in_=w2_raw[:, 2 * KP * b:2 * KP * (b + 1)].rearrange("p (m t e) -> p t m e", t=PACK, e=2))

        def deal_w2_scales(b):
            nc.vector.tensor_copy(
                out=w2_s[:, KP * b:KP * (b + 1)].rearrange("p (t m) -> p t m", t=PACK),
                in_=w2_s_raw[:, KP * b:KP * (b + 1)].rearrange("p (m t) -> p t m", t=PACK))

        def quantise(grouped, name):
            codes = keep.tile([P, KP], U32, name=name + "_w", align_bytes=64)
            scales = keep.tile([P, KP], U8, name=name + "_s", align_bytes=64)
            nc.vector.quantize_mx(out=codes[:].bitcast(FP8X4), scales=scales[:], in_=grouped[:])
            return codes, scales

        def make_w1(b):
            grouped = keep.tile([P, PACK * KP], BF16, name="w1_bf%d" % b, tag="w_bf", bufs=3, align_bytes=64)
            nc.scalar.copy(out=grouped[:].rearrange("p (t m j) -> p m t j", t=PACK, j=PACK),
                           in_=w1_raw[b][:].rearrange("p j (m t) -> p m t j", t=PACK))
            codes, scales = quantise(grouped, "w1_%d" % b)
            w1_w.append(codes)
            w1_s.append(scales)

        def make_w3(b):
            raw = load_w(w3, b, slice(0, N), "w3_raw%d" % b)
            grouped = keep.tile([P, PACK * KP], BF16, name="w3_bf%d" % b, tag="w_bf", bufs=3, align_bytes=64)
            nc.scalar.copy(out=grouped[:].rearrange("p (c i j) -> p c j i", i=4, j=PACK),
                           in_=raw[:].rearrange("p j (c i) -> p c j i", i=4))
            codes, scales = quantise(grouped, "w3_%d" % b)
            w3_w.append(codes)
            w3_s.append(scales)

        make_w1(0)
        deal_w2_words(0)
        deal_w2_scales(0)
        neg_gain = keep.tile([P, 2, PACK], F32, name="neg_gain")
        v_w = []
        for hf in range(2):
            vw = keep.tile([P, HALF], U32, name="v_w%d" % hf, align_bytes=64)
            nc.vector.tensor_copy(vw[:], tab_w[:].indirect(half_list(lst1, hf)))
            v_w.append(vw)
            if hf == 0:
                nc.vector.tensor_scalar_mul(neg_gain[:], gain_sb[:], -1.0)
        stage = [keep.tile([P, 2 * HALF], F32, name="stage%d" % hf, align_bytes=64) for hf in range(2)]

        hs = {}

        def make_h(i, hf):
            b, t = divmod(i, PACK)
            if hf == 0 and i == 7:
                hs[i] = keep.tile([P, S], F32, name="h7", align_bytes=64)
            elif hf == 0:
                hs[i] = keep.tile([P, S], F32, name="h%d" % i, tag="h", bufs=3, align_bytes=64)
            h = hs[i]
            rows = slice(t * P, (t + 1) * P)
            a_ps = psum.tile([P, HALF], F32, name="a_ps")
            b_ps = psum.tile([P, HALF], F32, name="b_ps")
            for jj in range(4):
                js = slice(jj * P, (jj + 1) * P)
                vs = v_s[:, hf * HALF + jj * P: hf * HALF + (jj + 1) * P]
                nc.tensor.matmul_mx(out=a_ps[:, js], lhsT=v_w[hf][:, js].bitcast(FP8X4), lhsT_scale=vs,
                                    rhs=w1_w[b][:, rows].bitcast(FP8X4), rhs_scale=w1_s[b][:, rows],
                                    start=True, stop=True)
            for jj in range(4):
                js = slice(jj * P, (jj + 1) * P)
                vs = v_s[:, hf * HALF + jj * P: hf * HALF + (jj + 1) * P]
                c0 = b * KP + t * P
                nc.tensor.matmul_mx(out=b_ps[:, js], lhsT=v_w[hf][:, js].bitcast(FP8X4), lhsT_scale=vs,
                                    rhs=w2_w[:, 2 * c0:2 * (c0 + P)].bitcast(FP4X4), rhs_scale=w2_s[:, c0:c0 + P],
                                    start=True, stop=True)
            a_t = stage[hf][:, 0:HALF]
            b_t = stage[hf][:, HALF:2 * HALF]
            nc.scalar.activation(a_t, a_ps[:], ACT.Copy, scale=-1.0)
            nc.scalar.activation(b_t, b_ps[:], ACT.Abs)
            h_ps = psum.tile([P, HALF], F32, name="h_ps", tag="h_ps")
            for jj in range(4):
                js = slice(jj * P, (jj + 1) * P)
                nc.tensor.matmul(h_ps[:, js], lhsT=a_t[:, js], rhs=ident[:], is_transpose=True, start=True, stop=False)
                nc.tensor.matmul(h_ps[:, js], lhsT=b_t[:, js], rhs=ident[:], is_transpose=True, start=False, stop=True)
            nc.scalar.activation(h[:, hf * HALF:(hf + 1) * HALF], h_ps[:], ACT.Copy, scale=neg_gain[:, b, t:t + 1])

        def make_first_h(hf):
            js = slice(hf * HALF, (hf + 1) * HALF)
            tag = ("out_ps", "h_ps")[hf]
            a_ps = psum.tile([P, HALF], F32, name="a_first", tag=tag)
            b_ps = psum.tile([P, HALF], F32, name="b_first", tag=tag)
            nc.tensor.matmul_mx(out=a_ps[:], lhsT=w1_w[0][:, 0:P].bitcast(FP8X4), lhsT_scale=w1_s[0][:, 0:P],
                                rhs=v_w[hf][:].bitcast(FP8X4), rhs_scale=v_s[:, js], start=True, stop=True)
            nc.tensor.matmul_mx(out=b_ps[:], lhsT=w2_w[:, 0:2 * P].bitcast(FP4X4), lhsT_scale=w2_s[:, 0:P],
                                rhs=v_w[hf][:].bitcast(FP8X4), rhs_scale=v_s[:, js], start=True, stop=True)
            gain_a = stage[hf][:, 0:HALF]
            abs_b = stage[hf][:, HALF:2 * HALF]
            nc.scalar.activation(gain_a, a_ps[:], ACT.Copy, scale=gain_sb[:, 0, 0:1])
            nc.scalar.activation(abs_b, b_ps[:], ACT.Abs)
            nc.vector.scalar_tensor_tensor(out=hs[0][:, js], in0=abs_b, scalar=neg_gain[:, 0, 0:1], in1=gain_a,
                                           op0=ALU.mult, op1=ALU.add)

        hs[0] = keep.tile([P, S], F32, name="h0", tag="h", bufs=3, align_bytes=64)
        make_first_h(0)
        make_first_h(1)

        planes = {}
        x_late = keep.tile([P, PACK * HALF], BF16, name="x_late", align_bytes=64)
        x_w, x_s = {}, {}

        def plane_tile(b, hf):
            if (b, hf) not in planes:
                planes[(b, hf)] = keep.tile([P, PACK, HALF], BF16, name="planes%d%d" % (b, hf), tag="planes", bufs=2, align_bytes=64)
            return planes[(b, hf)]

        def add_bias(i, hf, picked):
            b, t = divmod(i, PACK)
            if (b, hf) == (1, 0):
                dst = x_late[:].rearrange("p (n t) -> p t n", t=PACK)[:, t, :]
            else:
                dst = plane_tile(b, hf)[:, t, :]
            nc.scalar.activation(dst, picked, ACT.Identity, bias=bx_sb[:, b, t:t + 1])

        def make_x(b, hf):
            grouped = keep.tile([P, PACK * HALF], BF16, name="x_bf%d%d" % (b, hf), tag="x_bf", bufs=2, align_bytes=64)
            nc.scalar.copy(out=grouped[:].rearrange("p (c i t) -> p c t i", i=4, t=PACK),
                           in_=planes[(b, hf)][:].rearrange("p t (c i) -> p c t i", i=4))
            x_w[(b, hf)], x_s[(b, hf)] = quantise(grouped, "x_%d%d" % (b, hf))

        drill = []

        def load_page1(nt):
            tag, bufs = ("w_rows", 2) if nt < 2 else ("page", 7)
            pg = keep.tile([P, T2], F32, name="drill%d" % nt, tag=tag, bufs=bufs, align_bytes=64)
            nc.sync.dma_start(out=pg[:], in_=page1[nt * P:(nt + 1) * P, :])
            drill.append(pg)

        def put_h(i):
            t = i % PACK
            if i == 0:
                for hf in range(2):
                    js = slice(hf * HALF, (hf + 1) * HALF)
                    nc.vector.tensor_tensor(pages[i][:].indirect(half_list(lst2, hf)), hs[i][:, js], wgs_sb[t][:, js], ALU.mult)
            else:
                nc.vector.tensor_tensor(pages[i][:].indirect(lst2[:]), hs[i][:], wgs_sb[t], ALU.mult)

        def pick_x(i):
            if i < PACK:
                nc.vector.tensor_copy(stage[1][:], pages[i][:].indirect(lst3[:]))
                for hf in range(2):
                    add_bias(i, hf, stage[1][:, hf * HALF:(hf + 1) * HALF])
            else:
                picked = stage[1][:, (i % 2) * HALF:(i % 2 + 1) * HALF]
                nc.vector.tensor_copy(picked, pages[i][:].indirect(half_list(lst3, 0)))
                add_bias(i, 0, picked)
            if i == 0:
                pages.append(load_page0(7))

        qw = []

        def make_q(nt):
            ns = slice(nt * P, (nt + 1) * P)
            q1 = keep.tile([P, S], F32, name="q1_%d" % nt, align_bytes=64)
            for hf in range(2):
                js = slice(hf * HALF, (hf + 1) * HALF)
                q_ps = psum.tile([P, HALF], F32, name="q_ps", tag="out_ps")
                nc.tensor.matmul_mx(out=q_ps[:], lhsT=w4_w[:, ns].bitcast(FP8X4), lhsT_scale=w4_s[:, ns],
                                    rhs=v_w[hf][:].bitcast(FP8X4), rhs_scale=v_s[:, js], start=True, stop=True)
                nc.scalar.activation(q1[:, js], q_ps[:], ACT.Copy, bias=1.0)
            return q1

        def make_qw(q1, dst):
            nc.vector.tensor_tensor(dst, q1[:], wgo_sb[:], ALU.mult)
            qw.append(dst)

        make_h(1, 0)
        make_h(1, 1)
        put_h(0)
        deal_w2_words(1)
        deal_w2_scales(1)
        make_w1(1)
        make_h(2, 0)
        make_h(2, 1)
        put_h(1)
        for i in range(2, 8):
            if i < 7:
                make_h(i + 1, 0)
            if i in (6, 7):
                make_x(0, i - 6)
            pick_x(i - 2)
            if i < 7:
                make_h(i + 1, 1)
            put_h(i)
        for nt in range(3):
            q1 = make_q(nt)
            make_qw(q1, q1[:])
        q1_last = make_q(3)
        make_w3(0)
        make_w3(1)
        for nt in range(4):
            load_page1(nt)
        pick_x(6)
        pick_x(7)

        x_w[(1, 0)], x_s[(1, 0)] = quantise(x_late, "x_10")
        late_b = x_late[:].bitcast(F32)
        late = [hs[7][:, 0:HALF], hs[7][:, HALF:S], late_b[:, 0:HALF], late_b[:, HALF:S]]
        for t in range(4):
            nc.vector.tensor_copy(late[t], pages[4 + t][:].indirect(half_list(lst3, 1)))
        make_qw(q1_last, wgs_sb[3])

        def put_y(nt, hf):
            ns = slice(nt * P, (nt + 1) * P)
            js = slice(hf * HALF, (hf + 1) * HALF)
            m_ps = psum.tile([P, HALF], F32, name="m_ps", tag="h_ps")
            for b in range(2):
                nc.tensor.matmul_mx(out=m_ps[:], lhsT=w3_w[b][:, ns].bitcast(FP8X4), lhsT_scale=w3_s[b][:, ns],
                                    rhs=x_w[(b, hf)][:].bitcast(FP8X4), rhs_scale=x_s[(b, hf)][:],
                                    start=(b == 0), stop=(b == 1))
            m_sb = keep.tile([P, HALF], F32, name="m_sb", tag="m_sb", bufs=3, align_bytes=64)
            nc.scalar.copy(m_sb[:], m_ps[:])
            nc.vector.tensor_tensor(drill[nt][:].indirect(half_list(lst4, hf)), m_sb[:], qw[nt][:, js], ALU.mult)

        put_y(0, 0)
        put_y(1, 0)
        for t in range(4):
            add_bias(4 + t, 1, late[t])
        make_x(1, 1)
        put_y(2, 0)
        for nt in range(4):
            if nt == 1:
                put_y(3, 0)
            put_y(nt, 1)
            nc.sync.dma_start(out=out[nt * P:(nt + 1) * P, :], in_=drill[nt][:])
